import numpy as np, ml_dtypes
CORES = [25,29,65,69,153,157,193,197]
N = 8
import mx_ref
BF = ml_dtypes.bfloat16
def gcols(t, e):
    v = np.concatenate([t.reshape(8, 16, -1, 4), np.zeros((8, 16, 1, 4), BF)], axis=2)
    return np.ascontiguousarray(np.stack([v[g][:, e[g]] for g in range(8)])).reshape(128, -1)
def tile(rs):
    return np.stack(rs, axis=2).reshape(128, -1).astype(BF)
def pick(q, e):
    c = np.concatenate([q[0].reshape(128, -1, 4), np.zeros((128, 1, 4), np.uint8)], axis=1); s = np.concatenate([q[1], np.ones((16, 1), np.uint8)], axis=1)
    return (np.ascontiguousarray(c[:, e].reshape(128, -1)), np.ascontiguousarray(s[:, e]))
def join(*qs):
    return (np.concatenate([q[0] for q in qs], axis=1), np.concatenate([q[1] for q in qs], axis=1))
def put(q, e, v):
    c, s = q[0].reshape(128, -1, 4).copy(), q[1].copy(); c[:, e] = v[0].reshape(128, -1, 4); s[:, e] = v[1]
    return (c.reshape(128, -1), s)
def pk(c, s):
    return (np.ascontiguousarray(c), mx_ref.live(s))
def emit(q):
    return q[0], q[1]
def packed(v, rng):
    q = [mx_ref.quantize(np.ascontiguousarray(v[r])) for r in range(N)]
    return np.stack([a for a, b in q]), np.stack([mx_ref.plane(b, rng) for a, b in q])
def values_of_codes():
    e, c = np.zeros((128, 128, 4), np.float32), np.zeros((128, 2, 4), np.uint8)
    e[np.arange(128), np.arange(128), 0] = 1
    c[:127, :, 0] = np.arange(256).reshape(2, 128).T[:127]
    return mx_ref.matmul(mx_ref.quantize(e.reshape(128, 512).astype(BF)), (c.reshape(128, 8), np.full((16, 2), 127, np.uint8))).T.reshape(-1).astype(np.float64)
CODE_VALUE, SCALE_VALUE = values_of_codes(), 2.0 ** (np.arange(256) - 127.0)
def decode(q):
    return (CODE_VALUE[q[0]].reshape(16, 8, -1, 4) * SCALE_VALUE[q[1]][:, None, :, None] + 0.0).reshape(128, -1).astype(np.float32)
def f(rng, *shape):
    return mx_ref.flush((rng.standard_normal(shape, dtype=np.float32) * np.exp2(rng.integers(-2, 3, shape[:-1] + (1,)))).astype(BF))
def wide(rng, *shape, cols=0):
    v = rng.standard_normal(shape, dtype=np.float32) * np.exp2(rng.integers(-12, 13, shape)).astype(np.float32)
    if cols: v *= np.repeat(np.exp2(rng.integers(-cols, cols + 1, shape[:-2] + (1, shape[-1] // 4))) * (rng.random(shape[:-2] + (1, shape[-1] // 4)) > 0.0625), 4, axis=-1).astype(np.float32)
    return mx_ref.flush(v.astype(BF))
C, R = 320, 2
STEP = [1, 4]
def maxima(p):
    h = p[::16]
    m = np.zeros((8, C), bool)
    m[:, 1:-1] = (h[:, 1:-1] > h[:, :-2]) & (h[:, 1:-1] >= h[:, 2:])
    return m
def brackets(m):
    j = np.arange(C)
    a = np.maximum.accumulate(np.where(m, j, -1), axis=1)
    b = np.full((8, C), C - 1)
    b[:, :-1] = np.minimum.accumulate(np.where(m, j, C - 1)[:, ::-1], axis=1)[:, ::-1][:, 1:]
    return a, b, np.where(a[:, -1:] < 0, C - 1, a[:, -1:])
def half(s, t):
    return ((s.astype(np.float32) + t.astype(np.float32)) * np.float32(0.5)).astype(BF)
def numbers_of(rng):
    return {"x": np.array(f(rng, N, 128, 4 * C)), "u": np.array(f(rng, N, 128, 512)), "v": np.array(f(rng, N, 128, 512))}
def weights(rng, still=[]):
    w = np.array(f(rng, N, 128, 2048)).reshape(N, 8, 16, 4, 8, 16, 4)
    for i in still:
        w[:, :, i] = 0
        w[:, :, :, :, :, i] = 0
    c, p = packed(w.reshape(N, 128, 2048), rng)
    return {"wc": c, "ws": p}
def signs(rng):
    return np.stack([rng.permutation(8) % 2 * 2.0 - 1.0 for r in range(N)])
def setup_inputs(rng):
    return {**numbers_of(rng), **weights(rng)}
def setup_inputs_ties(rng):
    d = numbers_of(rng)
    e = rng.permutation(N)
    x = d["x"].reshape(N, 8, 16, C, 4)
    for r in range(N):
        k = np.zeros(C, int) if r == e[0] else rng.permutation(C) % 3
        a = x[r][:, :8, :3].copy()
        a[:, :, 2] = 0
        x[r][:, :8] = a[:, :, k]
    x[e[1]] = 0
    u = d["u"].reshape(N, 8, 16, 8, 16, 4)
    k = u.copy()
    u[:, :, :, :, 0] = 0
    for g in range(8): u[:, g, :8, g, 0] = k[:, g, :8, g, 0]
    return {"x": x.reshape(N, 128, 4 * C), "u": u.reshape(N, 128, 512), "v": d["v"], **weights(rng, range(8))}
def setup_inputs_near(rng):
    d = numbers_of(rng)
    x = d["x"].astype(np.float32).reshape(N, 8, 16, C, 4)
    u = d["u"].reshape(N, 128, 128, 4)
    u[:, :, ::16] = 0
    x[:, :, 0] = 0
    x[:, :, 8] = 0
    o, c = rng.permutation(N) % 4, signs(rng)
    for r in range(N):
        q = 2.0 ** -23 if o[r] < 2 else 2.0 ** -26
        if o[r] < 2: x[r, :, 0, :, 0] = c[r][:, None]
        s = rng.integers(0, 4, (8, C))
        s[:, :13] = [0, 2, 3, 3, 2, 2, 0, 1, 0, 1, 2, 0, 3]
        x[r, :, 8, :, 0] = s * q
        x[r, :, 9:] = rng.integers(4, 8, (8, 7, C, 4)) * q
        if o[r] == 3: x[r, :, 9, :, 0] = s * q
        k = 1.0 if o[r] % 2 == 0 else 2.0 ** -30
        for h in range(0, 128, 16):
            u[r, h, h, 0] = k
            u[r, h + 8, h, 0] = k
            if o[r] == 3:
                u[r, h + 8, h, 0] = 1.125 * k
                u[r, h + 9, h, 0] = -k
    return {"x": x.reshape(N, 128, 4 * C).astype(BF), "u": u.reshape(N, 128, 512), "v": d["v"], **weights(rng, [0, 8, 9, 10, 11, 12, 13, 14, 15])}
def setup_inputs_shapes(rng):
    d = numbers_of(rng)
    x = d["x"].astype(np.float32).reshape(N, 8, 16, C, 4)
    u = d["u"].reshape(N, 128, 128, 4)
    x[:, :, :11] = 0
    x[:, :, :8] = (9 + 4 * rng.integers(0, 2, (N, 8, 8, C, 4))) * np.exp2(-8.0 - np.arange(32).reshape(8, 1, 4) % 13)
    x[:, :, 0, :, 0] = 1.96875
    u[:, :, ::16] = 0
    j = np.arange(C)
    n = np.stack([rng.permutation(8) for r in range(N)])
    n[1] = n[0]
    size = np.where(rng.permutation(N) < N // 2, 2.0 ** -30, 1.0) * np.where(rng.permutation(N) < N // 2, -1.0, 1.0)
    for r in range(N):
        m = (1, C - 2)[r % 2]
        key = np.stack([0 * j + 5, j, C - 1 - np.abs(j - m), np.abs(j - m), j % 2, j // 2, (C - 1 - j) // 3, ((j == 1) | (j == C - 2)) + 0])[n[r]]
        z = ((key[:, :, None] >> np.arange(12)) & 1) * np.exp2(np.arange(12.0))
        for i in range(3): x[r, :, 8 + i] = z[:, :, 4 * i:4 * i + 4]
        for h in range(0, 128, 16): u[r, h + 8:h + 11, h] = size[r]
    return {"x": x.reshape(N, 128, 4 * C).astype(BF), "u": u.reshape(N, 128, 512), "v": d["v"], **weights(rng, range(11))}
def setup_inputs_huge(rng):
    d = numbers_of(rng)
    x = 0.55 + 0.35 * rng.random((N, 128, C, 4))
    a = 2.0 ** 30 * (1 - 0.1 * rng.random((N, 128, 8, 4))) * signs(rng)[:, None, :, None]
    h = np.where(np.arange(128) < 64, 1.0, -1.0)
    for r in rng.permutation(N)[:N // 2]:
        c = rng.permutation(C) % 2 * 2.0 - 1.0
        x[r] = 0.7 + 0.05 * rng.random((128, C, 4)) + 0.15 * h[:, None, None] * c[:, None]
        a[r] *= h[:, None, None]
    u = d["u"].reshape(N, 128, 128, 4)
    u[:, :, ::16] = a.astype(np.float32).astype(BF)
    w = np.zeros((N, 128, 4, 128, 4), np.float32)
    i = np.arange(128)
    for b in range(4): w[:, i, b, i, b] = 0.125
    wc, ws = packed(w.reshape(N, 128, 2048).astype(BF), rng)
    return {"x": (x * 2.0 ** 30).astype(np.float32).reshape(N, 128, 4 * C).astype(BF), "u": u.reshape(N, 128, 512), "v": d["v"], "wc": wc, "ws": ws}
def setup_inputs_spread(rng):
    d = setup_inputs(rng)
    d["x"] = wide(rng, N, 128, 4 * C, cols=6)
    return d
def check_inputs(d):
    b = []
    for k in ("x", "u", "v"):
        a = np.abs(d[k].astype(np.float32))
        if not (np.isfinite(a).all() and ((a == 0) | (a >= 2.0 ** -30) & (a <= 2.0 ** 30)).all()): b.append("a value of " + k)
    if ((d["wc"] & 0x7F) == 0x7F).any(): b.append("a code of wc that is no number")
    z = np.zeros((128, 4, 4), np.float32)
    z[:, 1] = 2.0 ** -30
    z[:, 2] = 2.0 ** 30
    c, s = emit(mx_ref.quantize(z.reshape(128, 16).astype(BF)))
    for r in range(N):
        p = mx_ref.live(d["ws"][r])
        if not ((p == s[0, 0]) | (p >= s[0, 1]) & (p <= s[0, 2])).all(): b.append("a scale of ws")
    return b
def reference(x, u, v, wc, ws):
    qu = [mx_ref.quantize(u[r]) for r in range(N)]
    lay = [pk(wc[r], ws[r]) for r in range(N)]
    now = [x[r] for r in range(N)]
    om = np.zeros((N, 8, C), np.float32)
    for t in range(R):
        full, ends, four, rest, sent = [], [], [], [], []
        for r in range(N):
            q = mx_ref.quantize(now[r])
            p = mx_ref.matmul(qu[r], q)
            hi, lo = maxima(p), maxima(-p)
            a, b, i = brackets(hi)
            c, d, k = brackets(lo)
            full.append(decode(q).astype(BF))
            ends.append(gcols(full[r], np.concatenate([i, k], axis=1)))
            four.append((np.where(a < 0, C, a), b, np.where(c < 0, C + 1, c), d))
            om[r] = 1.0 + hi - lo
        for r in range(N):
            z = np.concatenate([full[r], ends[(r - 1) % N]], axis=1)
            a, b, c, d = [gcols(z, k) for k in four[r]]
            e = half(half(a, b), half(c, d))
            rest.append((full[r].astype(np.float32) - e.astype(np.float32)).astype(BF))
            sent.append(mx_ref.quantize(e))
        now = [tile([mx_ref.matmul(pick(lay[r], np.arange(128 * b, 128 * b + 128)), sent[r ^ STEP[t]]) * np.float32(0.03125) + rest[r][:, b::4].astype(np.float32) for b in range(4)]) for r in range(N)]
    y = np.zeros((N, 128, C), np.float32)
    oc, osc = np.zeros((N, 128, 4 * C), np.uint8), np.zeros((N, 16, C), np.uint8)
    for r in range(N):
        q = mx_ref.quantize(now[r])
        y[r] = mx_ref.matmul(mx_ref.quantize(v[r]), q)
        oc[r], osc[r] = emit(q)
    return {"y": y, "om": om, "oc": oc, "osc": osc}

from concourse.bass import DstId, RemoteDMATransfer
from concourse.mybir import dt, AluOpType, ActivationFunctionType

C = 320
H = 160
STEP = [1, 4]
BF, F32, I32, U16, U8, X4 = "bfloat16", "float32", "int32", "uint16", "uint8", "float8_e4m3fn_x4"


def _s(n, d):
    return ("sbuf", [128, n], d)


SCRATCH = {
    "ps": ("psum", [128, 4096], F32),
    "X0": _s(1296, BF), "X1": _s(1296, BF), "X2": _s(1296, BF), "X32": _s(1280, BF),
    "ut": _s(512, BF), "vt": _s(512, BF),
    "qu": _s(128, X4), "su": _s(128, U8), "qu2": _s(128, X4), "su2": _s(128, U8), "qv": _s(128, X4), "sv": _s(128, U8),
    "qw": _s(512, X4), "sw": _s(512, U8),
    "QX0": _s(328, X4), "QX1": _s(328, X4), "QX2": _s(320, X4),
    "SX0": _s(352, U8), "SX1": _s(352, U8), "SX2": _s(320, U8),
    "J": _s(514, BF), "Za": _s(514, BF), "Zb": _s(514, BF), "Zq": _s(512, BF), "qk": _s(640, X4), "sk": _s(640, U8),
    "A16": _s(8, I32), "P16": _s(1, I32), "P17": _s(1, I32), "vv": _s(1, I32), "pa16": _s(1, I32), "s4": _s(1, I32),
    "tc": _s(1, F32), "fc": _s(1, F32), "y9": _s(1, F32), "w9": _s(2, I32), "rot": _s(2, I32), "ec": _s(2, F32),
    "sgb": _s(1, BF), "uoff": _s(8, U16), "cidx": _s(2, U16),
    "N": _s(C, BF), "up": _s(C, BF), "dn": _s(C, BF),
    "pq": _s(C, F32), "pd": _s(C, BF), "rise": _s(C, BF), "flat": _s(336, BF), "rr": _s(C, BF), "nz": _s(C, BF),
    "AB": _s(704, BF), "O": _s(1520, BF),
    "eoff": _s(2, U16), "offa": _s(32, U16), "offb": _s(32, U16), "offi0": _s(32, U16), "offi1": _s(32, U16),
    "ET": _s(512, BF), "QT0": _s(128, X4), "ST0": _s(128, U8), "QT1": _s(128, X4), "ST1": _s(128, U8),
    "RC0": _s(8, X4), "RS0": _s(32, U8), "RC1": _s(8, X4), "RS1": _s(32, U8),
    "Q": _s(1344, BF), "tp": _s(1280, BF), "W": _s(1280, BF), "tf": _s(1280, BF), "E": _s(1280, BF),
    "G": _s(1280, BF), "G32": _s(1280, BF),
    "QE0": _s(C, X4), "SE0": _s(C, U8), "QE1": _s(C, X4), "SE1": _s(C, U8),
    "LE0": _s(C, X4), "LS0": _s(C, U8), "LE1": _s(C, X4), "LS1": _s(C, U8),
    "ysb": _s(C, F32), "upT": _s(C, BF), "mx": _s(20, BF), "mn": _s(20, BF), "OT": _s(C, F32), "val": _s(C, F32),
}
SEMAPHORES = ["cv", "cs", "ct", "cg", "lx", "lu", "lw", "lws", "lv", "sent", "end0", "end1", "rel0", "rel1",
              "a00", "a01", "a10", "a11", "om1", "st0", "st1", "st2"]

A = AluOpType
COPY = ActivationFunctionType.Copy


def _bits(engs):
    return sum(1 << e for e in engs)


def _relays(src, dst, T, topo):
    if topo.may_write(src, dst):
        return None
    c = [k for k in topo.cores_of(src) if T.rank_of(k) is None and topo.may_write(k, dst)]
    c.sort(key=lambda k: topo.die(k) != topo.die(src))
    return c[:2]


def _send_ends(g, src, dsts, sc, ss, dc, ds, sem, T, topo):
    e = topo.engines(src, dsts[0])
    h = len(e) // 2
    to = [[DstId(rid=r, pnc=p)] for r, p in (topo.addr(d, src) for d in dsts)]
    g.remote_dma_fused([
        RemoteDMATransfer(dst_ids=to[0], dma_engine_mask=_bits(e[:h]), remote_sem=sem, src=sc.bitcast(dt.uint8), dst=dc.bitcast(dt.uint8)),
        RemoteDMATransfer(dst_ids=to[1], dma_engine_mask=_bits(e[h:]), remote_sem=sem, src=ss, dst=ds),
    ], local_sem=T.sem.sent)
    return len(e)


def rank_program(g, core, T, topo):
    rank = T.rank_of(core)
    cores = list(T.cores)
    n = len(cores)
    if rank is None:
        for r in range(n):
            src, dst = cores[r], cores[(r + 1) % n]
            rel = _relays(src, dst, T, topo)
            if rel is not None and core in rel:
                rid, pid = topo.addr(dst, core)
                for t in range(2):
                    g.wait_ge(T.sem["rel%d" % t], len(topo.engines(src, core)) // 2)
                    if core == rel[0]:
                        a, b = T["QX%d" % t][:, 320:328].bitcast(dt.uint8), T["RC%d" % t][:].bitcast(dt.uint8)
                    else:
                        a, b = T["SX%d" % t][:, 320:328], T["RS%d" % t][:, 0:8]
                    g.remote_dma(a, b, T.sem["end%d" % t], T.sem.sent, pid, rid, topo.mask(core, dst))
                g.wait_ge(T.sem.sent, 2 * len(topo.engines(core, dst)))
        return

    Qs = {"g": g, "v": g.vector, "s": g.scalar, "t": g.tensor, "y": g.sync}
    own = {"g": "cg", "v": "cv", "s": "cs", "t": "ct"}
    count = {}
    clock = {k: {} for k in Qs}
    writer, readers = {}, {}

    def wait(q, tok):
        sem, val, clk = tok
        if clock[q].get(sem, 0) >= val:
            return
        Qs[q].wait_ge(T.sem[sem], val)
        for k, v in clk.items():
            if clock[q].get(k, 0) < v:
                clock[q][k] = v

    def op(q, fn, rd=(), wr=(), sem=None, inc=1):
        deps = []
        for k in rd:
            if k in writer:
                deps.append(writer[k])
            if k.startswith("bank"):
                deps += [tk for (qq, tk) in readers.get(k, []) if qq != q]
        for k in wr:
            if k in writer:
                deps.append(writer[k])
            deps += [tk for (qq, tk) in readers.get(k, [])]
        deps.sort(key=lambda tk: -tk[1])
        for tk in deps:
            wait(q, tk)
        sem = sem or own[q]
        count[sem] = count.get(sem, 0) + inc
        fn().then_inc(T.sem[sem], inc)
        clk = dict(clock[q])
        clk[sem] = count[sem]
        tok = (sem, count[sem], clk)
        for k in rd:
            readers.setdefault(k, []).append((q, tok))
        for k in wr:
            writer[k] = tok
            readers[k] = []
        return tok

    def need(q, keys):
        for k in keys:
            wait(q, writer[k])

    def arrives(key, sem, val):
        count[sem] = val
        writer[key] = (sem, val, {sem: val})

    V, S, PE, Y = g.vector, g.scalar, g.tensor, g.sync

    def bank(b, a=0, e=C):
        return T.ps[:, 512 * b + a:512 * b + e]

    def ts(out, in0, s1, s2, o0, o1, rd, wr):
        if o1 is None:
            return op("v", lambda: V.tensor_scalar(out, in0, s1, None, o0), rd, wr)
        return op("v", lambda: V.tensor_scalar(out, in0, s1, s2, o0, o1), rd, wr)

    def tt(out, in0, in1, o, rd, wr):
        return op("v", lambda: V.tensor_tensor(out, in0, in1, o), rd, wr)

    def act(out, in_, rd, wr, scale=None):
        if scale is None:
            return op("s", lambda: S.activation(out, in_, COPY), rd, wr)
        return op("s", lambda: S.activation(out, in_, COPY, scale=scale), rd, wr)

    def quant(qc, sc, in_, rd, wr):
        return op("v", lambda: V.quantize_mx(qc, sc, in_), rd, wr)

    def mm(out, lc, ls, rc, rs, rd, wr):
        return op("t", lambda: PE.matmul_mx(out, lc, ls, rc, rs, True, True), rd, wr)

    def iota(out, pat, base, mult, wr, flt=False):
        if flt:
            return op("g", lambda: g.iota(out, pat, base, mult, allow_small_or_imprecise_dtypes=True), (), wr)
        return op("g", lambda: g.iota(out, pat, base, mult), (), wr)

    def fill(ap, wr):
        return op("v", lambda: V.memset(ap, 0.0), (), wr)

    def scan(out, d0, d1, init, rd, wr):
        return op("v", lambda: V.tensor_tensor_scan(out, d0, d1, init, A.add, A.min), rd, wr)

    op("y", lambda: Y.dma_start(T.X0[:, 16:1296], T.x[:]), (), ["X0_0"], "lx", 16)
    op("s", lambda: S.dma_start(T.ut[:], T.u[:]), (), ["ut"], "lu", 16)
    iota(T.J[:], [[1, 514]], 0, -4, ["J"], True)
    iota(T.A16[:], [[16, 8]], 0, 0, ["A16"])
    iota(T.P16[:], [[0, 1]], 0, 16, ["P16"])
    iota(T.P17[:], [[0, 1]], 0, 17, ["P17"])
    iota(T.N[:], [[1, C]], -H, 0, ["N"], True)
    iota(T.AB[:, 0:32], [[0, 32]], 0, 0, ["ABp0"], True)
    iota(T.AB[:, 671:704], [[0, 33]], 0, 0, ["ABp1"], True)
    iota(T.O[:, 1344:1520], [[0, 176]], 0, 0, ["Op"], True)
    for b in range(4):
        iota(T.Q[:, 336 * b:336 * b + 16], [[0, 16]], 0, 0, ["Qp%d" % b], True)

    fill(T.rise[:, 0:1], ["rise0"])
    fill(T.flat[:, 320:321], ["flatp"])
    fill(T.X0[:, 0:12], ["X0z"])
    fill(T.X1[:, 0:12], ["X1z"])
    fill(T.ET[:, 32:512], ["ETz"])
    fill(T.OT[:], ["OTz"])
    ts(T.Za[:], T.J[:], 2.0, None, A.is_equal, None, ["J"], ["Za"])
    ts(T.Zb[:], T.J[:], 3.0, None, A.is_equal, None, ["J"], ["Zb"])
    for b, z, o in ((0, "Za", 2), (2, "Za", 0), (1, "Zb", 2), (3, "Zb", 0)):
        quant(T.qk[:, 128 * b:128 * b + 128], T.sk[:, 128 * b:128 * b + 128], T[z][:, o:o + 512], [z], ["qk%d" % b])
    op("v", lambda: V.tensor_copy(T.uoff[:], T.A16[:]), ["A16"], ["uoff"])
    quant(T.qu[:], T.su[:], T.ut[:], ["ut"], ["qu"])
    ts(T.s4[:], T.P16[:], 64, None, A.bitwise_and, None, ["P16"], ["s4"])
    op("v", lambda: V.tensor_copy(T.qu2[:].bitcast(dt.uint32), T.qu[:].bitcast(dt.uint32).indirect(T.uoff[:])), ["qu", "uoff"], ["qu2"])
    act(T.su2[:], T.su[:].indirect(T.uoff[:]), ["qu", "uoff"], ["su2"])
    ts(T.vv[:], T.P16[:], 240, None, A.bitwise_and, None, ["P16"], ["vv"])
    ts(T.pa16[:], T.P17[:], 16, None, A.bitwise_and, None, ["P17"], ["pa16"])
    act(T.up[:], T.N[:], ["N"], ["up"], 1.0 / 512)
    act(T.dn[:], T.N[:], ["N"], ["dn"], -1.0 / 512)

    need("y", ["X0_0"])
    op("y", lambda: Y.dma_start(T.qw[:].bitcast(dt.uint8), T.wc[:]), (), ["qw"], "lw", 16)
    op("y", lambda: Y.dma_start(T.sw[:], T.ws[:]), (), ["sw"], "lws", 16)
    op("y", lambda: Y.dma_start(T.vt[:], T.v[:]), (), ["vt"], "lv", 16)

    right, left = cores[(rank + 1) % n], cores[(rank - 1) % n]
    out_to = _relays(core, right, T, topo)
    in_by = _relays(left, core, T, topo)
    sent = [0]

    for t in range(2):
        X, Xn = T["X%d" % t], T["X%d" % (t + 1)]
        QX, SX = T["QX%d" % t], T["SX%d" % t]
        xk, xn, qx = "X%d" % t, "X%d" % (t + 1), ["QX%d_0" % t, "QX%d_1" % t]
        xa = ["X0_0"] if t == 0 else [xk + "_%d%d" % (h, b) for h in range(2) for b in range(4)]
        partner = cores[rank ^ STEP[t]]
        arrives("ends%d" % t, "end%d" % t, sum(len(topo.engines(k, core)) for k in (in_by or [left])))
        for h in range(2):
            arrives("LE%d%d" % (t, h), "a%d%d" % (t, h), 2 * len(topo.engines(partner, core)))

        if t == 0:
            quant(QX[:, 0:C], SX[:, 0:C], X[:, 16:1296], xa, qx)
        act(X[:, 12:16], X[:, 1292:1296], xa, [xk + "p"])
        mm(bank(4), T.qu2[:], T.su2[:], QX[:, 0:C], SX[:, 0:C], ["qu2", "su2"] + qx, ["bank4"])
        if t == 0:
            ts(T.sgb[:], T.s4[:], -1.0 / 32, 1.0, A.mult, A.add, ["s4"], ["sgb"])
            ts(T.y9[:], T.vv[:], 0.5625, None, A.mult, None, ["vv"], ["y9"])
            ts(T.tc[:], T.vv[:], 160.0, -156.0, A.is_ge, A.mult, ["vv"], ["tc"])
            ts(T.w9[:], T.A16[:, 0:2], T.y9[:], None, A.add, None, ["A16", "y9"], ["w9"])
            act(T.Zq[:], T.Za[:, 2:514], ["Za"], ["Zq"], 0.25)
        for b in range(4):
            mm(bank(b), T.qk[:, 128 * b:128 * b + 128], T.sk[:, 128 * b:128 * b + 128], QX[:, 0:C], SX[:, 0:C],
               ["qk%d" % b] + qx, ["bank%d" % b])
        for b in range(4):
            act(T.Q[:, 336 * b + 16:336 * b + 336], bank(b), ["bank%d" % b], ["Q%d" % b], 0.25)

        op("v", lambda: V.tensor_copy(T.pq[:], bank(4)), ["bank4"], ["pq"])
        if t == 0:
            ts(T.rot[:], T.w9[:], 3, 3, A.arith_shift_right, A.bitwise_and, ["w9"], ["rot"])
        tt(T.pd[:, 1:C], bank(4, 1, C), T.pq[:, 0:C - 1], A.subtract, ["bank4", "pq"], ["pd"])
        if t == 0:
            ts(T.ec[:], T.rot[:], 656.0, 1.0 / 2048, A.add, A.mult, ["rot"], ["ec"])
        ts(T.rise[:, 1:C], T.pd[:, 1:C], T.sgb[:], 0.0, A.mult, A.is_gt, ["pd", "sgb"], ["rise"])
        ts(T.flat[:, 1:C], T.pd[:, 1:C], T.sgb[:], 0.0, A.mult, A.is_le, ["pd", "sgb"], ["flat"])
        scan(T.rr[:], T.rise[:], T.up[:], -161.0 / 512, ["rise", "rise0", "up"], ["rr"])
        scan(T.AB[:, 32:352], T.flat[:, 1:321], T.rr[:], -161.0 / 512, ["flat", "flatp", "rr"], ["a"])
        ts(T.eoff[:], T.ec[:], T.AB[:, 351:352], 2048.0, A.add, A.mult, ["ec", "a"], ["eoff"])
        op("v", lambda: V.tensor_copy(T.ET[:, 0:32], X[:].indirect(T.eoff[:])), xa + [xk + "p", xk + "z", "eoff"], ["ET"])
        QT, ST = T["QT%d" % t], T["ST%d" % t]
        quant(QT[:], ST[:], T.ET[:], ["ET", "ETz"], ["QT%d" % t])
        need("g", ["QT%d" % t])
        if out_to is None:
            sent[0] += _send_ends(g, core, [right, right], QT[:, 0:8], ST[:, 0:32], QX[:, 320:328], SX[:, 320:352], T.sem["end%d" % t], T, topo)
        else:
            sent[0] += _send_ends(g, core, out_to, QT[:, 0:8], ST[:, 0:32], T["RC%d" % t][:], T["RS%d" % t][:], T.sem["rel%d" % t], T, topo)

        scan(T.nz[:, 319:0:-1], T.flat[:, 320:1:-1], T.dn[:, 319:0:-1], -159.0 / 512, ["flat", "flatp", "dn"], ["nz"])
        if t == 0:
            ts(T.fc[:], T.pa16[:], 21.0, None, A.mult, None, ["pa16"], ["fc"])
        scan(T.AB[:, 670:351:-1], T.rise[:, 319:0:-1], T.nz[:, 319:0:-1], -159.0 / 512, ["rise", "nz"], ["b"])
        if t == 0:
            ts(T.cidx[:, 0:1], T.vv[:], T.tc[:], T.fc[:], A.add, A.add, ["vv", "tc", "fc"], ["cidx0"])
            ts(T.cidx[:, 1:2], T.vv[:], T.fc[:], 100.0, A.add, A.add, ["vv", "fc"], ["cidx1"])
        ab = ["a", "b", "ABp0", "ABp1"]
        op("v", lambda: V.transpose(T.O[:, 0:320], T.AB[:, 32:672:2]), ab, ["O4"])
        op("v", lambda: V.transpose(T.O[:, 320:672], T.AB[:, 0:704:2]), ab, ["O3"])
        op("v", lambda: V.transpose(T.O[:, 672:992], T.AB[:, 32:352]), ab, ["O2"])
        ci = ["cidx0", "cidx1", "O4", "O3", "O2"]
        ts(T.offb[:], T.O[:, 160:848].indirect(T.cidx[:]), -512.0, 176.0, A.mult, A.add, ci, ["offb"])
        op("v", lambda: V.transpose(T.O[:, 992:1344], T.AB[:, 16:368]), ab, ["O1"])
        ts(T.offa[:], T.O[:, 0:688].indirect(T.cidx[:]), 512.0, 176.0, A.mult, A.add, ci, ["offa"])
        for h in range(2):
            ts(T["offi%d" % h][:], T.O[:, 672 + H * h:1360 + H * h].indirect(T.cidx[:]), 256.0, 80.25, A.mult, A.add,
               ci + ["O1", "Op"], ["offi%d" % h])
        if t == 0:
            quant(T.qk[:, 512:640], T.sk[:, 512:640], T.Zq[:], ["Zq"], ["qk4"])

        for b in range(4):
            win = T.Q[:, 336 * b:336 * b + 336]
            qk = ["Q%d" % b, "Qp%d" % b]
            act(T.tp[:, C * b:C * b + C], win.indirect(T.offb[:, 0:20]), qk + ["offb"], ["tp%d" % b])
            tt(T.W[:, C * b:C * b + C], win.indirect(T.offa[:, 0:20]), T.tp[:, C * b:C * b + C], A.add,
               qk + ["offa", "tp%d" % b], ["W%d" % b])
        mm(bank(4, 0, 128), T.qk[:, 512:640], T.sk[:, 512:640], QX[:, 200:328], SX[:, 200:328], ["qk4", "ends%d" % t] + qx, ["bank4"])
        wk = ["W%d" % b for b in range(4)]
        tt(T.W[:, 0:1280:H], bank(4, 120, 128), T.W[:, 0:1280:H], A.add, ["bank4"] + wk, wk)

        QE, SE, LE, LS = T["QE%d" % t], T["SE%d" % t], T["LE%d" % t], T["LS%d" % t]
        rid, pid = topo.addr(partner, core)
        for h in range(2):
            off = T["offi%d" % h]
            for b in range(4):
                tf = T.tf[:, 640 * h + H * b:640 * h + H * b + H]
                act(tf, T.W[:, C * b + H:C * b + C].indirect(off[:, 10:20]), ["W%d" % b, "offi%d" % h], ["tf%d%d" % (h, b)])
                tt(T.E[:, 640 * h + b:640 * h + 640:4], T.W[:, C * b:C * b + H].indirect(off[:, 0:10]), tf, A.add,
                   ["W%d" % b, "offi%d" % h, "tf%d%d" % (h, b)], ["E%d%d" % (h, b)])
            cs = slice(H * h, H * h + H)
            quant(QE[:, cs], SE[:, cs], T.E[:, 640 * h:640 * h + 640], ["E%d%d" % (h, b) for b in range(4)], ["QE%d%d" % (t, h)])
            need("g", ["QE%d%d" % (t, h)])
            sem = T.sem["a%d%d" % (t, h)]
            m = topo.mask(core, partner)
            g.remote_dma(LE[:, cs].bitcast(dt.uint8), QE[:, cs].bitcast(dt.uint8), sem, T.sem.sent, pid, rid, m)
            g.remote_dma(LS[:, cs], SE[:, cs], sem, T.sem.sent, pid, rid, m)
            sent[0] += 2 * len(topo.engines(core, partner))

        for h in range(2):
            for b in range(4):
                tt(T.G[:, 640 * h + H * b:640 * h + H * b + H], bank(b, H * h, H * h + H), T.E[:, 640 * h + b:640 * h + 640:4],
                   A.subtract, ["bank%d" % b, "E%d%d" % (h, b)], ["G%d%d" % (h, b)])
            act(T.G32[:, 640 * h:640 * h + 640], T.G[:, 640 * h:640 * h + 640], ["G%d%d" % (h, b) for b in range(4)], ["G32_%d" % h], 32.0)
        if t == 0:
            quant(T.qv[:], T.sv[:], T.vt[:], ["vt"], ["qv"])
            op("v", lambda: V.transpose(T.upT[:], T.up[:]), ["up"], ["upT"])
        else:
            tt(T.mx[:], T.O[:, 672:992:16], T.upT[:, 0:C:16], A.is_equal, ["O2", "upT"], ["mx"])
            tt(T.mn[:], T.O[:, 676:992:16], T.upT[:, 0:C:16], A.not_equal, ["O2", "upT"], ["mn"])
            tt(T.OT[:, 0:C:16], T.mx[:], T.mn[:], A.add, ["mx", "mn", "OTz"], ["OT"])
            op("v", lambda: V.transpose(T.val[:], T.OT[:]), ["OT", "OTz"], ["val"])
            op("y", lambda: Y.dma_start(T.om[:], T.val[0:128:16, :]), ["val"], (), "om1", 16)

        QN, SN = T["QX%d" % (t + 1)], T["SX%d" % (t + 1)]
        for h in range(2):
            cs = slice(H * h, H * h + H)
            for b in range(4):
                k = b + 4 * (1 - h)
                mm(bank(k, 0, H), T.qw[:, 128 * b:128 * b + 128], T.sw[:, 128 * b:128 * b + 128], LE[:, cs], LS[:, cs],
                   ["qw", "sw", "LE%d%d" % (t, h)], ["bank%d" % k])
            if t == 1 and h == 1:
                mm(bank(4, 0, H), T.qv[:], T.sv[:], QN[:, 0:H], SN[:, 0:H], ["qv", "QX2_0"], ["bank4"])
            for b in range(4):
                k = b + 4 * (1 - h)
                src = T.X32[:, 640 * h + H * b:640 * h + H * b + H]
                dst = Xn[:, 16 + 640 * h + b:656 + 640 * h:4]
                tt(src, bank(k, 0, H), T.G32[:, 640 * h + H * b:640 * h + H * b + H], A.add,
                   ["bank%d" % k, "G32_%d" % h], ["X32_%d%d" % (h, b)])
                if b < 3:
                    act(dst, src, ["X32_%d%d" % (h, b)], [xn + "_%d%d" % (h, b)], 0.03125)
                else:
                    ts(dst, src, 0.03125, None, A.mult, None, ["X32_%d%d" % (h, b)], [xn + "_%d%d" % (h, b)])
            qn = "QX%d_%d" % (t + 1, h)
            quant(QN[:, cs], SN[:, cs], Xn[:, 16 + 640 * h:656 + 640 * h], [xn + "_%d%d" % (h, b) for b in range(4)], [qn])
            if t == 0:
                continue
            if h == 1:
                act(T.ysb[:, 0:H], bank(4, 0, H), ["bank4"], ["y0"])
                op("y", lambda: Y.dma_start(T.y[:, 0:H], T.ysb[:, 0:H]), ["y0"], (), "st0", 16)
            op("y", lambda: Y.dma_start(T.oc[:, 640 * h:640 * h + 640], QN[:, cs].bitcast(dt.uint8)), [qn], (), "st0", 16)
            if h == 1:
                mm(bank(5, 0, H), T.qv[:], T.sv[:], QN[:, cs], SN[:, cs], ["qv", qn], ["bank5"])
                op("v", lambda: V.tensor_copy(T.ysb[:, cs], bank(5, 0, H)), ["bank5"], ["y1"])
                for k in range(4):
                    e, q = ((Y, "y"), (S, "s"))[k % 2]
                    op(q, lambda: e.dma_start(T.osc[4 * k:4 * k + 4, :], SN[32 * k:32 * k + 4, :]), ["QX2_0", qn], (), "st%d" % (1 + k % 2), 16)
                op("s", lambda: S.dma_start(T.y[:, cs], T.ysb[:, cs]), ["y1"], (), "st2", 16)

    count["sent"] = sent[0]
    for sem, val in count.items():
        g.wait_ge(T.sem[sem], val)
